import numpy as np
import ml_dtypes


def mxq(x, axis, fmt="e4m3"):
    dtype, down = {"e4m3": (ml_dtypes.float8_e4m3fn, 7), "e5m2": (ml_dtypes.float8_e5m2, 14)}[fmt]
    v = np.moveaxis(np.asarray(x, np.float32).astype(ml_dtypes.bfloat16).astype(np.float64), axis, -1)
    blocks = v.reshape(v.shape[:-1] + (-1, 32))
    amax = np.abs(blocks).max(-1, keepdims=True)
    byte = np.maximum(np.where(amax > 0, np.frexp(amax)[1] - 1 + 127, 0) - down, 1)
    scale = np.exp2(byte - 127.0)
    codes = (blocks / scale).astype(np.float32).astype(dtype).astype(np.float64)
    return np.moveaxis((codes * scale).reshape(v.shape), -1, axis)


WIDE = False


def mx_kscale(k):
    if not WIDE:
        return np.ones(k)
    levels = np.array([10, -10, 5, -5, 0])
    if k % 512:
        return np.exp2(np.random.permutation(np.resize(levels, k // 32))).repeat(32)
    a = np.empty((k // 512, 16))
    for p in range(k // 512):
        a[p, :8] = np.random.permutation(np.resize(levels, 8))
        for g in range(8):
            far = levels[np.abs(levels - a[p, g]) >= 10]
            a[p, g + 8] = far[np.random.randint(len(far))]
    return np.exp2(a.ravel()).repeat(32)


def f64(x):
    return np.asarray(x).astype(np.float64)


def striped(idx):
    return np.tile(idx.reshape(-1, 16).T, (8, 1)).astype(np.uint16)


def unstriped(offs):
    return offs[:16].T.reshape(-1).astype(np.int64)


def silu(v):
    return v / (1.0 + np.exp(-np.maximum(v, -700.0)))


K, T, E, C, H, N = 512, 768, 4, 128, 1024, 384


def by_expert(wq, xq):
    return np.concatenate([wq[e].T @ xq[:, e * C:(e + 1) * C] for e in range(E)], axis=1)


def setup_inputs():
    n = np.random.standard_normal
    s = mx_kscale(K)[:, None]
    u = mx_kscale(H)
    return {
        "xT": (n((K, T)) * s).astype(np.float32),
        "w1": (n((E, K, H)) / np.sqrt(K) / s[None]).astype(np.float32),
        "w3": (n((E, K, H)) / np.sqrt(K) / s[None] * u[None, None, :]).astype(np.float32),
        "w2": (n((E, H, N)) / np.sqrt(H) / u[None, :, None]).astype(np.float32),
        "gate": np.tile(np.random.uniform(0.2, 1.0, E * C), (N, 1)).astype(np.float32),
        "offs": striped(np.random.permutation(T)[:E * C]),
    }


def reference(xT, w1, w3, w2, gate, offs):
    idx = unstriped(offs)
    xq = mxq(f64(xT)[:, idx], 0, "e4m3")
    h = silu(by_expert(mxq(f64(w1), 1, "e4m3"), xq))
    h = h * by_expert(mxq(f64(w3), 1, "e4m3"), xq)
    y = by_expert(mxq(f64(w2), 1, "e4m3"), mxq(h, 0, "e4m3"))
    out = np.zeros((N, T))
    out[:, idx] = f64(gate) * y
    return out

@@ -1,0 +1,213 @@
+from contextlib import ExitStack
+
+import concourse.mybir as mybir
+
+K, T, E, C, H, N = 512, 768, 4, 128, 1024, 384
+S = E * C
+P = 128
+PACK = 4
+HB = 512
+U = H // HB
+NB = N // P
+
+FLOPS = 2 * K * H * S * 2 + 2 * H * N * S
+
+F32 = mybir.dt.float32
+BF16 = mybir.dt.bfloat16
+U32 = mybir.dt.uint32
+U16 = mybir.dt.uint16
+U8 = mybir.dt.uint8
+X4 = mybir.dt.float8_e4m3fn_x4
+MULT = mybir.AluOpType.mult
+SILU = mybir.ActivationFunctionType.Silu
+V_SHARE = 40
+V_SHARE_LAST = 40
+LAG_Q, LAG_S, LAG_M, LAG_P = 1, 1, 1, 1
+TAIL = 3
+
+def tile_routed_moe_kernel(tc, xT, w1, w3, w2, gate, offs, out):
+    nc = tc.nc
+    with ExitStack() as ctx:
+        held = ctx.enter_context(tc.tile_pool(name="held", bufs=1))
+        raw = ctx.enter_context(tc.tile_pool(name="raw", bufs=1))
+        work = ctx.enter_context(tc.tile_pool(name="work", bufs=1))
+        psum = ctx.enter_context(tc.psum_pool(name="psum", bufs=1))
+
+        offsets = held.tile([P, S // 16], U16, name="offsets")
+        x_codes = held.tile([P, T], U32, name="x_codes", align_bytes=64)
+        x_scales = held.tile([P, T], U8, name="x_scales", align_bytes=64)
+        g_codes = held.tile([P, S], U32, name="g_codes", align_bytes=64)
+        g_scales = held.tile([P, S], U8, name="g_scales", align_bytes=64)
+        gates = held.tile([P, NB, S], F32, name="gates")
+        warm = held.tile([P, 1], F32, name="warm")
+        windows = [held.tile([P, T], F32, name=f"window{b}") for b in range(NB)]
+
+        def cast(engine, dst, src):
+            if engine == "V":
+                nc.vector.tensor_copy(out=dst, in_=src)
+            else:
+                nc.scalar.copy(out=dst, in_=src)
+
+        def quantize(codes, scales, grouped):
+            nc.vector.quantize_mx(out=codes.bitcast(X4), scales=scales, in_=grouped)
+
+        def multiply(dst, l_codes, l_scales, r_codes, r_scales, start, stop):
+            nc.tensor.matmul_mx(out=dst, lhsT=l_codes.bitcast(X4), lhsT_scale=l_scales,
+                                rhs=r_codes.bitcast(X4), rhs_scale=r_scales, start=start, stop=stop)
+
+        x_view = xT.rearrange("(p j) n -> p j n", j=PACK)
+        x_parts = [(0, 256, [("V", 0, 256)]), (256, 512, [("S", 256, 512), ("V", 0, 256)])]
+        x_raw = []
+        for n0, width, eng in x_parts:
+            t = raw.tile([P, PACK, width], F32, name=f"x_raw{n0}")
+            nc.sync.dma_start(out=t[:], in_=x_view[:, :, n0:n0 + width])
+            x_raw.append(t)
+            if n0 == 0:
+                nc.sync.dma_start(offsets[:], offs)
+
+        items = []
+        for e in range(E):
+            items += [("up", e, 0, 0), ("up", e, 1, 0), ("up", e, 0, 1), ("up", e, 1, 1)]
+            if e == 0:
+                items += [("gate",)]
+            items += [("down", e, 0, 0, N)]
+            items += [("down", e, 1, 0, N)] if e < E - 1 else [("down", e, 1, 0, 256), ("down", e, 1, 256, 384)]
+        up_raw, down_raw = {}, {}
+        for item in items:
+            if item[0] == "up":
+                kind, e, m, u = item
+                t = raw.tile([P, PACK, HB], F32, tag="up", bufs=10)
+                nc.sync.dma_start(out=t[:], in_=(w1, w3)[m][e].rearrange("(p j) c -> p j c", j=PACK)[:, :, u * HB:(u + 1) * HB])
+                up_raw[e, m, u] = t
+            elif item[0] == "gate":
+                nc.sync.dma_start(out=gates[:], in_=gate.rearrange("(b p) s -> p b s", p=P))
+            else:
+                kind, e, u, n0, n1 = item
+                if e not in down_raw:
+                    down_raw[e] = raw.tile([P, U, PACK, N], F32, tag="down", bufs=2, name="down_r")
+                nc.sync.dma_start(out=down_raw[e][:, u, :, n0:n1], in_=w2[e].rearrange("(u p j) n -> p u j n", u=U, j=PACK)[:, u, :, n0:n1])
+        items = [item for item in items if item[0] != "gate"]
+
+        nc.vector.memset(warm[:], 0.0)
+        nc.scalar.activation(out=warm[:], in_=warm[:], func=SILU)
+        nc.gpsimd.memset(x_scales[:], 0)
+        for window in windows:
+            nc.vector.memset(window[:], 0.0)
+
+        for (n0, width, eng), t in zip(x_parts, x_raw):
+            xb = work.tile([P, width, PACK], BF16, name=f"x_b{n0}", align_bytes=64)
+            for which, a, b in eng:
+                cast(which, xb[:, a:b, :].rearrange("p (c i) j -> p c j i", i=4), t[:, :, a:b].rearrange("p j (c i) -> p c j i", i=4))
+            quantize(x_codes[:, n0:n0 + width], x_scales[:, n0:n0 + width], xb[:].rearrange("p n j -> p (n j)"))
+        nc.vector.tensor_copy(g_codes[:], x_codes[:].indirect(offsets[:]))
+        nc.vector.tensor_copy(g_scales[:], x_scales[:].indirect(offsets[:]))
+
+        up_codes, banks, acts, h_codes, down_codes, down_b, up_b, done = {}, {}, {}, {}, {}, {}, {}, {}
+
+        def cast_up(e, m, u):
+            share = V_SHARE if e < E - 1 else V_SHARE_LAST
+            b = work.tile([P, PACK, P, PACK], BF16, tag="up_b", bufs=6, align_bytes=64)
+            t = up_raw[e, m, u]
+            for eng, m0, m1 in (("S", share, P), ("V", 0, share)):
+                if m1 > m0:
+                    cast(eng, b[:, :, m0:m1, :].rearrange("p t m j -> p m j t"),
+                         t[:, :, 4 * m0:4 * m1].rearrange("p j (m t) -> p m j t", t=4))
+            up_b[e, m, u] = b
+
+        def quantize_up(e, m, u):
+            codes = work.tile([P, HB], U32, tag=f"c{m}{u}", bufs=2, align_bytes=64)
+            scales = work.tile([P, HB], U8, tag=f"s{m}{u}", bufs=2, align_bytes=64)
+            quantize(codes[:], scales[:], up_b[e, m, u][:].rearrange("p t m j -> p (t m j)"))
+            up_codes[e, m, u] = codes, scales
+
+        def multiply_up(e, u):
+            slots = slice(e * C, (e + 1) * C)
+            for m in range(2):
+                bank = psum.tile([P, PACK, C], F32, tag=f"bank{m}", bufs=2)
+                codes, scales = up_codes[e, m, u]
+                for t in range(PACK):
+                    cols = slice(t * P, (t + 1) * P)
+                    multiply(bank[:, t, :], codes[:, cols], scales[:, cols], g_codes[:, slots], g_scales[:, slots], True, True)
+                banks[e, m, u] = bank
+
+        def activate(e, u):
+            act = work.tile([P, C, PACK], F32, tag="act", bufs=2)
+            nc.scalar.activation(out=act[:], in_=banks[e, 0, u][:].rearrange("p t n -> p n t"), func=SILU)
+            acts[e, u] = act
+
+        def hidden(e, u):
+            hb = work.tile([P, C, PACK], BF16, tag="hb", bufs=2, align_bytes=64)
+            nc.vector.tensor_tensor(hb[:], banks[e, 1, u][:].rearrange("p t n -> p n t"), acts[e, u][:], MULT)
+            codes = work.tile([P, C], U32, tag=f"hc{u}", bufs=2, align_bytes=64)
+            scales = work.tile([P, C], U8, tag=f"hs{u}", bufs=2, align_bytes=64)
+            quantize(codes[:], scales[:], hb[:].rearrange("p n t -> p (n t)"))
+            h_codes[e, u] = codes, scales
+
+        def cast_down(e, eng, u, n0, n1):
+            if e not in down_b:
+                down_b[e] = work.tile([P, U * N, PACK], BF16, tag="down_b", bufs=2, align_bytes=64, name="down_bt")
+            cast(eng, down_b[e][:, u * N + n0:u * N + n1, :].rearrange("p (c i) j -> p c j i", i=4),
+                 down_raw[e][:, u, :, n0:n1].rearrange("p j (c i) -> p c j i", i=4))
+
+        def quantize_down(e, a0, a1):
+            if e not in down_codes:
+                c2 = work.tile([P, U * N], U32, tag="c2", bufs=2, align_bytes=64)
+                s2 = work.tile([P, U * N], U8, tag="s2", bufs=2, align_bytes=64)
+                down_codes[e] = c2, s2
+            c2, s2 = down_codes[e]
+            quantize(c2[:, a0:a1], s2[:, a0:a1], down_b[e][:, a0:a1, :].rearrange("p n j -> p (n j)"))
+
+        def project(e, blocks):
+            slots = slice(e * C, (e + 1) * C)
+            c2, s2 = down_codes[e]
+            y = psum.tile([P, NB, C], F32, tag="y", bufs=2)
+            for nb in blocks:
+                for u in range(U):
+                    cols = slice(u * N + nb * P, u * N + (nb + 1) * P)
+                    hc, hs = h_codes[e, u]
+                    multiply(y[:, nb, :], c2[:, cols], s2[:, cols], hc[:], hs[:], u == 0, u == U - 1)
+            ys = work.tile([P, NB, C], F32, tag="ys", bufs=2)
+            b0, b1 = blocks[0], blocks[-1] + 1
+            nc.scalar.copy(out=ys[:, b0:b1, :], in_=y[:, b0:b1, :])
+            for nb in blocks:
+                nc.vector.tensor_tensor(windows[nb][:].indirect(offsets[:, e * C // 16:(e + 1) * C // 16]), ys[:, nb, :], gates[:, nb, slots], MULT)
+                if e == LAST_DOWN:
+                    nc.sync.dma_start(out=out[nb * P:(nb + 1) * P, :], in_=windows[nb][:])
+
+        LAST_DOWN = items[-1][1]
+        agenda = {}
+
+        def at(step, rank, call):
+            agenda.setdefault((step, rank), []).append(call)
+
+        for k, item in enumerate(items):
+            tail = k >= len(items) - TAIL
+            lag_q, lag_s, lag_m, lag_p = (0, 0, 0, 0) if tail else (LAG_Q, LAG_S, LAG_M, LAG_P)
+            if item[0] == "up":
+                kind, e, m, u = item
+                at(k, 0, lambda e=e, m=m, u=u: cast_up(e, m, u))
+                q = k + lag_q
+                at(q, 2, lambda e=e, m=m, u=u: quantize_up(e, m, u))
+                done[e, m, u] = q
+                if (e, 1 - m, u) in done:
+                    q = max(q, done[e, 1 - m, u])
+                    at(q, 3, lambda e=e, u=u: multiply_up(e, u))
+                    s = q + lag_s
+                    at(s, 1 if s > q else 5, lambda e=e, u=u: activate(e, u))
+                    h = s + lag_m
+                    at(h, 1 if h > q else 6, lambda e=e, u=u: hidden(e, u))
+                    done[e, "h", u] = h
+            else:
+                kind, e, u, n0, n1 = item
+                eng = "V" if u == 1 and k < len(items) - 4 else "S"
+                at(k, 0, lambda e=e, eng=eng, u=u, n0=n0, n1=n1: cast_down(e, eng, u, n0, n1))
+                q = k + lag_q
+                pieces = [(0, 256), (256, 384)] if (n0, n1) == (0, N) else [(n0, n1)]
+                at(q, 2, lambda e=e, u=u, pieces=pieces: [quantize_down(e, u * N + a, u * N + b) for a, b in pieces])
+                done[e, "d", u] = q
+                if u == 1:
+                    p = max(q, done[e, "d", 0], done[e, "h", 0], done[e, "h", 1]) + lag_p
+                    at(p, 4 if p > q else 7, lambda e=e, n0=n0, n1=n1: project(e, list(range(n0 // P, n1 // P))))
+        for key in sorted(agenda):
+            for call in agenda[key]:
+                call()

@@ -20,10 +20,6 @@ U8 = mybir.dt.uint8
 X4 = mybir.dt.float8_e4m3fn_x4
 MULT = mybir.AluOpType.mult
 SILU = mybir.ActivationFunctionType.Silu
-V_SHARE = 40
-V_SHARE_LAST = 40
-LAG_Q, LAG_S, LAG_M, LAG_P = 1, 1, 1, 1
-TAIL = 3
 
 def tile_routed_moe_kernel(tc, xT, w1, w3, w2, gate, offs, out):
     nc = tc.nc
@@ -58,35 +54,49 @@ def tile_routed_moe_kernel(tc, xT, w1, w3, w2, gate, offs, out):
         x_view = xT.rearrange("(p j) n -> p j n", j=PACK)
         x_parts = [(0, 256, [("V", 0, 256)]), (256, 512, [("S", 256, 512), ("V", 0, 256)])]
         x_raw = []
-        for n0, width, eng in x_parts:
+
+        def load_x(n0, width):
             t = raw.tile([P, PACK, width], F32, name=f"x_raw{n0}")
             nc.sync.dma_start(out=t[:], in_=x_view[:, :, n0:n0 + width])
             x_raw.append(t)
-            if n0 == 0:
-                nc.sync.dma_start(offsets[:], offs)
 
-        items = []
-        for e in range(E):
-            items += [("up", e, 0, 0), ("up", e, 1, 0), ("up", e, 0, 1), ("up", e, 1, 1)]
-            if e == 0:
-                items += [("gate",)]
-            items += [("down", e, 0, 0, N)]
-            items += [("down", e, 1, 0, N)] if e < E - 1 else [("down", e, 1, 0, 256), ("down", e, 1, 256, 384)]
         up_raw, down_raw = {}, {}
-        for item in items:
-            if item[0] == "up":
-                kind, e, m, u = item
-                t = raw.tile([P, PACK, HB], F32, tag="up", bufs=10)
-                nc.sync.dma_start(out=t[:], in_=(w1, w3)[m][e].rearrange("(p j) c -> p j c", j=PACK)[:, :, u * HB:(u + 1) * HB])
-                up_raw[e, m, u] = t
-            elif item[0] == "gate":
-                nc.sync.dma_start(out=gates[:], in_=gate.rearrange("(b p) s -> p b s", p=P))
-            else:
-                kind, e, u, n0, n1 = item
-                if e not in down_raw:
-                    down_raw[e] = raw.tile([P, U, PACK, N], F32, tag="down", bufs=2, name="down_r")
-                nc.sync.dma_start(out=down_raw[e][:, u, :, n0:n1], in_=w2[e].rearrange("(u p j) n -> p u j n", u=U, j=PACK)[:, u, :, n0:n1])
-        items = [item for item in items if item[0] != "gate"]
+
+        def load_up(e, m, parts=1):
+            t = raw.tile([P, PACK, H], F32, tag="up", bufs=5)
+            view = (w1, w3)[m][e].rearrange("(p j) c -> p j c", j=PACK)
+            if parts == 1:
+                nc.sync.dma_start(out=t[:], in_=view)
+            up_raw[e, m] = t
+
+        def load_up_half(e, m, u):
+            cols = slice(u * HB, (u + 1) * HB)
+            if u == 0:
+                load_up(e, m, 2)
+            nc.sync.dma_start(out=up_raw[e, m][:, :, cols], in_=(w1, w3)[m][e].rearrange("(p j) c -> p j c", j=PACK)[:, :, cols])
+
+        def load_down(e):
+            t = raw.tile([P, U, PACK, N], F32, tag="down", bufs=2)
+            v = w2[e].rearrange("(u p j) n -> p u j n", u=U, j=PACK)
+            for u in range(U):
+                nc.sync.dma_start(out=t[:, u], in_=v[:, u])
+            down_raw[e] = t
+
+        load_x(0, 256)
+        nc.sync.dma_start(offsets[:], offs)
+        load_x(256, 512)
+        load_up(0, 0)
+        load_up(0, 1)
+        nc.sync.dma_start(out=gates[:], in_=gate.rearrange("(b p) s -> p b s", p=P))
+        load_down(0)
+        for e in range(1, E - 1):
+            load_up(e, 0)
+            load_up(e, 1)
+            load_down(e)
+        for u in range(U):
+            for m in range(2):
+                load_up_half(E - 1, m, u)
+        load_down(E - 1)
 
         nc.vector.memset(warm[:], 0.0)
         nc.scalar.activation(out=warm[:], in_=warm[:], func=SILU)
@@ -102,32 +112,34 @@ def tile_routed_moe_kernel(tc, xT, w1, w3, w2, gate, offs, out):
         nc.vector.tensor_copy(g_codes[:], x_codes[:].indirect(offsets[:]))
         nc.vector.tensor_copy(g_scales[:], x_scales[:].indirect(offsets[:]))
 
-        up_codes, banks, acts, h_codes, down_codes, down_b, up_b, done = {}, {}, {}, {}, {}, {}, {}, {}
+        up_codes, banks, acts, h_groups, h_codes, down_codes, down_b, up_b, ys_of, y_of = {}, {}, {}, {}, {}, {}, {}, {}, {}, {}
 
-        def cast_up(e, m, u):
-            share = V_SHARE if e < E - 1 else V_SHARE_LAST
-            b = work.tile([P, PACK, P, PACK], BF16, tag="up_b", bufs=6, align_bytes=64)
-            t = up_raw[e, m, u]
-            for eng, m0, m1 in (("S", share, P), ("V", 0, share)):
-                if m1 > m0:
-                    cast(eng, b[:, :, m0:m1, :].rearrange("p t m j -> p m j t"),
-                         t[:, :, 4 * m0:4 * m1].rearrange("p j (m t) -> p m j t", t=4))
-            up_b[e, m, u] = b
+        def cast_up(e, m, us, eng, m0, m1):
+            width = len(us) * P
+            key = (e, m, us)
+            if key not in up_b:
+                up_b[key] = work.tile([P, PACK, width, PACK], BF16, tag="up_b", bufs=4, align_bytes=64, name="up_bt")
+            t = up_raw[e, m]
+            c0 = us[0] * HB
+            if m1 > m0:
+                cast(eng, up_b[key][:, :, m0:m1, :].rearrange("p t m j -> p m j t"),
+                     t[:, :, c0 + 4 * m0:c0 + 4 * m1].rearrange("p j (m t) -> p m j t", t=4))
 
-        def quantize_up(e, m, u):
-            codes = work.tile([P, HB], U32, tag=f"c{m}{u}", bufs=2, align_bytes=64)
-            scales = work.tile([P, HB], U8, tag=f"s{m}{u}", bufs=2, align_bytes=64)
-            quantize(codes[:], scales[:], up_b[e, m, u][:].rearrange("p t m j -> p (t m j)"))
-            up_codes[e, m, u] = codes, scales
+        def quantize_up(e, m, us):
+            width = len(us) * HB
+            codes = work.tile([P, width], U32, tag=f"c{m}", bufs=2, align_bytes=64)
+            scales = work.tile([P, width], U8, tag=f"s{m}", bufs=2, align_bytes=64)
+            quantize(codes[:], scales[:], up_b[e, m, us][:].rearrange("p t m j -> p (t m j)"))
+            for i, u in enumerate(us):
+                up_codes[e, m, u] = [(codes[:, (t * len(us) + i) * P:(t * len(us) + i + 1) * P], scales[:, (t * len(us) + i) * P:(t * len(us) + i + 1) * P]) for t in range(PACK)]
 
         def multiply_up(e, u):
             slots = slice(e * C, (e + 1) * C)
             for m in range(2):
                 bank = psum.tile([P, PACK, C], F32, tag=f"bank{m}", bufs=2)
-                codes, scales = up_codes[e, m, u]
                 for t in range(PACK):
-                    cols = slice(t * P, (t + 1) * P)
-                    multiply(bank[:, t, :], codes[:, cols], scales[:, cols], g_codes[:, slots], g_scales[:, slots], True, True)
+                    codes, scales = up_codes[e, m, u][t]
+                    multiply(bank[:, t, :], codes, scales, g_codes[:, slots], g_scales[:, slots], True, True)
                 banks[e, m, u] = bank
 
         def activate(e, u):
@@ -135,19 +147,24 @@ def tile_routed_moe_kernel(tc, xT, w1, w3, w2, gate, offs, out):
             nc.scalar.activation(out=act[:], in_=banks[e, 0, u][:].rearrange("p t n -> p n t"), func=SILU)
             acts[e, u] = act
 
-        def hidden(e, u):
-            hb = work.tile([P, C, PACK], BF16, tag="hb", bufs=2, align_bytes=64)
-            nc.vector.tensor_tensor(hb[:], banks[e, 1, u][:].rearrange("p t n -> p n t"), acts[e, u][:], MULT)
-            codes = work.tile([P, C], U32, tag=f"hc{u}", bufs=2, align_bytes=64)
-            scales = work.tile([P, C], U8, tag=f"hs{u}", bufs=2, align_bytes=64)
-            quantize(codes[:], scales[:], hb[:].rearrange("p n t -> p (n t)"))
-            h_codes[e, u] = codes, scales
+        def gate_hidden(e, u):
+            if e not in h_groups:
+                h_groups[e] = work.tile([P, U, C, PACK], BF16, tag="hb", bufs=2, align_bytes=64, name="hb")
+                codes = work.tile([P, U * C], U32, tag="hc", bufs=2, align_bytes=64)
+                scales = work.tile([P, U * C], U8, tag="hs", bufs=2, align_bytes=64)
+                h_codes[e] = codes, scales
+            nc.vector.tensor_tensor(h_groups[e][:, u], banks[e, 1, u][:].rearrange("p t n -> p n t"), acts[e, u][:], MULT)
+
+        def quantize_hidden(e, u0, u1):
+            codes, scales = h_codes[e]
+            quantize(codes[:, u0 * C:u1 * C], scales[:, u0 * C:u1 * C], h_groups[e][:, u0:u1].rearrange("p u n t -> p (u n t)"))
 
         def cast_down(e, eng, u, n0, n1):
             if e not in down_b:
                 down_b[e] = work.tile([P, U * N, PACK], BF16, tag="down_b", bufs=2, align_bytes=64, name="down_bt")
-            cast(eng, down_b[e][:, u * N + n0:u * N + n1, :].rearrange("p (c i) j -> p c j i", i=4),
-                 down_raw[e][:, u, :, n0:n1].rearrange("p j (c i) -> p c j i", i=4))
+            if n1 > n0:
+                cast(eng, down_b[e][:, u * N + n0:u * N + n1, :].rearrange("p (c i) j -> p c j i", i=4),
+                     down_raw[e][:, u, :, n0:n1].rearrange("p j (c i) -> p c j i", i=4))
 
         def quantize_down(e, a0, a1):
             if e not in down_codes:
@@ -157,57 +174,88 @@ def tile_routed_moe_kernel(tc, xT, w1, w3, w2, gate, offs, out):
             c2, s2 = down_codes[e]
             quantize(c2[:, a0:a1], s2[:, a0:a1], down_b[e][:, a0:a1, :].rearrange("p n j -> p (n j)"))
 
-        def project(e, blocks):
-            slots = slice(e * C, (e + 1) * C)
+        def project(e, nb0, nb1):
             c2, s2 = down_codes[e]
+            hc, hs = h_codes[e]
             y = psum.tile([P, NB, C], F32, tag="y", bufs=2)
-            for nb in blocks:
+            for nb in range(nb0, nb1):
                 for u in range(U):
                     cols = slice(u * N + nb * P, u * N + (nb + 1) * P)
-                    hc, hs = h_codes[e, u]
-                    multiply(y[:, nb, :], c2[:, cols], s2[:, cols], hc[:], hs[:], u == 0, u == U - 1)
+                    h = slice(u * C, (u + 1) * C)
+                    multiply(y[:, nb, :], c2[:, cols], s2[:, cols], hc[:, h], hs[:, h], u == 0, u == U - 1)
+            y_of[e] = y
+
+        def copy_out(e, nb0, nb1):
+            slots = slice(e * C, (e + 1) * C)
             ys = work.tile([P, NB, C], F32, tag="ys", bufs=2)
-            b0, b1 = blocks[0], blocks[-1] + 1
-            nc.scalar.copy(out=ys[:, b0:b1, :], in_=y[:, b0:b1, :])
-            for nb in blocks:
-                nc.vector.tensor_tensor(windows[nb][:].indirect(offsets[:, e * C // 16:(e + 1) * C // 16]), ys[:, nb, :], gates[:, nb, slots], MULT)
-                if e == LAST_DOWN:
+            nc.vector.tensor_tensor(ys[:, nb0:nb1, :], y_of[e][:, nb0:nb1, :], gates[:, nb0:nb1, slots], MULT)
+            ys_of[e] = ys
+
+        def scatter(e, nb0, nb1):
+            slots = slice(e * C, (e + 1) * C)
+            for nb in range(nb0, nb1):
+                window = windows[nb][:].indirect(offsets[:, e * C // 16:(e + 1) * C // 16])
+                nc.vector.tensor_copy(window, ys_of[e][:, nb, :])
+                if e == E - 1:
                     nc.sync.dma_start(out=out[nb * P:(nb + 1) * P, :], in_=windows[nb][:])
 
-        LAST_DOWN = items[-1][1]
-        agenda = {}
+        BOTH = (0, 1)
+        for e in range(E - 1):
+            cast_up(e, 0, BOTH, "S", 64, 256)
+            cast_up(e, 0, BOTH, "V", 0, 64)
+            if e > 0:
+                copy_out(e - 1, 0, NB)
+            cast_up(e, 1, BOTH, "S", 64, 256)
+            quantize_up(e, 0, BOTH)
+            if e > 0:
+                scatter(e - 1, 0, NB)
+            cast_up(e, 1, BOTH, "V", 0, 64)
+            quantize_up(e, 1, BOTH)
+            multiply_up(e, 0)
+            multiply_up(e, 1)
+            cast_down(e, "S", 0, 0, N)
+            cast_down(e, "V", 1, 0, 128)
+            cast_down(e, "S", 1, 128, N)
+            activate(e, 0)
+            activate(e, 1)
+            quantize_down(e, 0, 512)
+            quantize_down(e, 512, 768)
+            gate_hidden(e, 0)
+            gate_hidden(e, 1)
+            quantize_hidden(e, 0, 2)
+            project(e, 0, NB)
 
-        def at(step, rank, call):
-            agenda.setdefault((step, rank), []).append(call)
+        e = E - 1
 
-        for k, item in enumerate(items):
-            tail = k >= len(items) - TAIL
-            lag_q, lag_s, lag_m, lag_p = (0, 0, 0, 0) if tail else (LAG_Q, LAG_S, LAG_M, LAG_P)
-            if item[0] == "up":
-                kind, e, m, u = item
-                at(k, 0, lambda e=e, m=m, u=u: cast_up(e, m, u))
-                q = k + lag_q
-                at(q, 2, lambda e=e, m=m, u=u: quantize_up(e, m, u))
-                done[e, m, u] = q
-                if (e, 1 - m, u) in done:
-                    q = max(q, done[e, 1 - m, u])
-                    at(q, 3, lambda e=e, u=u: multiply_up(e, u))
-                    s = q + lag_s
-                    at(s, 1 if s > q else 5, lambda e=e, u=u: activate(e, u))
-                    h = s + lag_m
-                    at(h, 1 if h > q else 6, lambda e=e, u=u: hidden(e, u))
-                    done[e, "h", u] = h
-            else:
-                kind, e, u, n0, n1 = item
-                eng = "V" if u == 1 and k < len(items) - 4 else "S"
-                at(k, 0, lambda e=e, eng=eng, u=u, n0=n0, n1=n1: cast_down(e, eng, u, n0, n1))
-                q = k + lag_q
-                pieces = [(0, 256), (256, 384)] if (n0, n1) == (0, N) else [(n0, n1)]
-                at(q, 2, lambda e=e, u=u, pieces=pieces: [quantize_down(e, u * N + a, u * N + b) for a, b in pieces])
-                done[e, "d", u] = q
-                if u == 1:
-                    p = max(q, done[e, "d", 0], done[e, "h", 0], done[e, "h", 1]) + lag_p
-                    at(p, 4 if p > q else 7, lambda e=e, n0=n0, n1=n1: project(e, list(range(n0 // P, n1 // P))))
-        for key in sorted(agenda):
-            for call in agenda[key]:
-                call()
+        def cast_half(m, u):
+            cast_up(e, m, (u,), "S", 48, P)
+            cast_up(e, m, (u,), "V", 0, 48)
+
+        cast_half(0, 0)
+        copy_out(e - 1, 0, NB)
+        quantize_up(e, 0, (0,))
+        cast_half(1, 0)
+        scatter(e - 1, 0, NB)
+        quantize_up(e, 1, (0,))
+        multiply_up(e, 0)
+        cast_half(0, 1)
+        activate(e, 0)
+        quantize_up(e, 0, (1,))
+        gate_hidden(e, 0)
+        quantize_hidden(e, 0, 1)
+        cast_half(1, 1)
+        quantize_up(e, 1, (1,))
+        multiply_up(e, 1)
+        cast_down(e, "S", 0, 0, N)
+        activate(e, 1)
+        quantize_down(e, 0, 256)
+        quantize_down(e, 256, 384)
+        gate_hidden(e, 1)
+        quantize_hidden(e, 1, 2)
+        cast_down(e, "S", 1, 0, 192)
+        cast_down(e, "V", 1, 192, N)
+        quantize_down(e, 384, 640)
+        quantize_down(e, 640, 768)
+        project(e, 0, NB)
+        copy_out(e, 0, NB)
+        scatter(e, 0, NB)

@@ -19,6 +19,10 @@ U16 = mybir.dt.uint16
 U8 = mybir.dt.uint8
 X4 = mybir.dt.float8_e4m3fn_x4
 MULT = mybir.AluOpType.mult
+V_SHARE = [40,40,40,40]
+DOWN_SHARE = [0,384]
+LAST_SHARE = [0,128,64]
+Y_BUFS = 4
 SILU = mybir.ActivationFunctionType.Silu
 
 def tile_routed_moe_kernel(tc, xT, w1, w3, w2, gate, offs, out):
@@ -62,41 +66,32 @@ def tile_routed_moe_kernel(tc, xT, w1, w3, w2, gate, offs, out):
 
         up_raw, down_raw = {}, {}
 
-        def load_up(e, m, parts=1):
-            t = raw.tile([P, PACK, H], F32, tag="up", bufs=5)
-            view = (w1, w3)[m][e].rearrange("(p j) c -> p j c", j=PACK)
-            if parts == 1:
-                nc.sync.dma_start(out=t[:], in_=view)
-            up_raw[e, m] = t
+        def load_up(e, m, u):
+            t = raw.tile([P, PACK, HB], F32, tag="up", bufs=10)
+            nc.sync.dma_start(out=t[:], in_=(w1, w3)[m][e].rearrange("(p j) c -> p j c", j=PACK)[:, :, u * HB:(u + 1) * HB])
+            up_raw[e, m, u] = t
 
-        def load_up_half(e, m, u):
-            cols = slice(u * HB, (u + 1) * HB)
-            if u == 0:
-                load_up(e, m, 2)
-            nc.sync.dma_start(out=up_raw[e, m][:, :, cols], in_=(w1, w3)[m][e].rearrange("(p j) c -> p j c", j=PACK)[:, :, cols])
-
-        def load_down(e):
-            t = raw.tile([P, U, PACK, N], F32, tag="down", bufs=2)
-            v = w2[e].rearrange("(u p j) n -> p u j n", u=U, j=PACK)
-            for u in range(U):
-                nc.sync.dma_start(out=t[:, u], in_=v[:, u])
-            down_raw[e] = t
+        def load_down(e, u, n0, n1):
+            if e not in down_raw:
+                down_raw[e] = raw.tile([P, U, PACK, N], F32, tag="down", bufs=2, name="down_r")
+            nc.sync.dma_start(out=down_raw[e][:, u, :, n0:n1], in_=w2[e].rearrange("(u p j) n -> p u j n", u=U, j=PACK)[:, u, :, n0:n1])
 
         load_x(0, 256)
         nc.sync.dma_start(offsets[:], offs)
-        load_x(256, 512)
-        load_up(0, 0)
-        load_up(0, 1)
-        nc.sync.dma_start(out=gates[:], in_=gate.rearrange("(b p) s -> p b s", p=P))
-        load_down(0)
-        for e in range(1, E - 1):
-            load_up(e, 0)
-            load_up(e, 1)
-            load_down(e)
-        for u in range(U):
-            for m in range(2):
-                load_up_half(E - 1, m, u)
-        load_down(E - 1)
+        for e in range(E):
+            for u in range(U):
+                for m in range(2):
+                    load_up(e, m, u)
+                    if (e, m, u) == (0, 0, 0):
+                        load_x(256, 512)
+            if e == 0:
+                nc.sync.dma_start(out=gates[:], in_=gate.rearrange("(b p) s -> p b s", p=P))
+            load_down(e, 0, 0, N)
+            if e < E - 1:
+                load_down(e, 1, 0, N)
+            else:
+                load_down(e, 1, 0, 256)
+                load_down(e, 1, 256, N)
 
         nc.vector.memset(warm[:], 0.0)
         nc.scalar.activation(out=warm[:], in_=warm[:], func=SILU)
@@ -104,43 +99,44 @@ def tile_routed_moe_kernel(tc, xT, w1, w3, w2, gate, offs, out):
         for window in windows:
             nc.vector.memset(window[:], 0.0)
 
-        for (n0, width, eng), t in zip(x_parts, x_raw):
+        x_b = []
+
+        def cast_x(i):
+            n0, width, shares = x_parts[i]
             xb = work.tile([P, width, PACK], BF16, name=f"x_b{n0}", align_bytes=64)
-            for which, a, b in eng:
-                cast(which, xb[:, a:b, :].rearrange("p (c i) j -> p c j i", i=4), t[:, :, a:b].rearrange("p j (c i) -> p c j i", i=4))
-            quantize(x_codes[:, n0:n0 + width], x_scales[:, n0:n0 + width], xb[:].rearrange("p n j -> p (n j)"))
-        nc.vector.tensor_copy(g_codes[:], x_codes[:].indirect(offsets[:]))
-        nc.vector.tensor_copy(g_scales[:], x_scales[:].indirect(offsets[:]))
+            for which, a, b in shares:
+                cast(which, xb[:, a:b, :].rearrange("p (c i) j -> p c j i", i=4), x_raw[i][:, :, a:b].rearrange("p j (c i) -> p c j i", i=4))
+            x_b.append(xb)
+
+        def quantize_x(i):
+            n0, width, shares = x_parts[i]
+            quantize(x_codes[:, n0:n0 + width], x_scales[:, n0:n0 + width], x_b[i][:].rearrange("p n j -> p (n j)"))
 
         up_codes, banks, acts, h_groups, h_codes, down_codes, down_b, up_b, ys_of, y_of = {}, {}, {}, {}, {}, {}, {}, {}, {}, {}
 
-        def cast_up(e, m, us, eng, m0, m1):
-            width = len(us) * P
-            key = (e, m, us)
-            if key not in up_b:
-                up_b[key] = work.tile([P, PACK, width, PACK], BF16, tag="up_b", bufs=4, align_bytes=64, name="up_bt")
-            t = up_raw[e, m]
-            c0 = us[0] * HB
-            if m1 > m0:
-                cast(eng, up_b[key][:, :, m0:m1, :].rearrange("p t m j -> p m j t"),
-                     t[:, :, c0 + 4 * m0:c0 + 4 * m1].rearrange("p j (m t) -> p m j t", t=4))
+        def cast_up(e, m, u):
+            b = work.tile([P, PACK, P, PACK], BF16, tag="up_b", bufs=6, align_bytes=64)
+            t = up_raw[e, m, u]
+            share = V_SHARE[e]
+            for eng, m0, m1 in (("S", share, P), ("V", 0, share)):
+                cast(eng, b[:, :, m0:m1, :].rearrange("p t m j -> p m j t"),
+                     t[:, :, 4 * m0:4 * m1].rearrange("p j (m t) -> p m j t", t=4))
+            up_b[e, m, u] = b
 
-        def quantize_up(e, m, us):
-            width = len(us) * HB
-            codes = work.tile([P, width], U32, tag=f"c{m}", bufs=2, align_bytes=64)
-            scales = work.tile([P, width], U8, tag=f"s{m}", bufs=2, align_bytes=64)
-            quantize(codes[:], scales[:], up_b[e, m, us][:].rearrange("p t m j -> p (t m j)"))
-            for i, u in enumerate(us):
-                up_codes[e, m, u] = [(codes[:, (t * len(us) + i) * P:(t * len(us) + i + 1) * P], scales[:, (t * len(us) + i) * P:(t * len(us) + i + 1) * P]) for t in range(PACK)]
+        def quantize_up(e, m, u):
+            codes = work.tile([P, HB], U32, tag=f"c{m}{u}", bufs=2, align_bytes=64)
+            scales = work.tile([P, HB], U8, tag=f"s{m}{u}", bufs=2, align_bytes=64)
+            quantize(codes[:], scales[:], up_b[e, m, u][:].rearrange("p t m j -> p (t m j)"))
+            up_codes[e, m, u] = codes, scales
 
-        def multiply_up(e, u):
+        def multiply_up(e, m, u):
             slots = slice(e * C, (e + 1) * C)
-            for m in range(2):
-                bank = psum.tile([P, PACK, C], F32, tag=f"bank{m}", bufs=2)
-                for t in range(PACK):
-                    codes, scales = up_codes[e, m, u][t]
-                    multiply(bank[:, t, :], codes, scales, g_codes[:, slots], g_scales[:, slots], True, True)
-                banks[e, m, u] = bank
+            bank = psum.tile([P, PACK, C], F32, tag=f"bank{m}", bufs=2)
+            codes, scales = up_codes[e, m, u]
+            for t in range(PACK):
+                cols = slice(t * P, (t + 1) * P)
+                multiply(bank[:, t, :], codes[:, cols], scales[:, cols], g_codes[:, slots], g_scales[:, slots], True, True)
+            banks[e, m, u] = bank
 
         def activate(e, u):
             act = work.tile([P, C, PACK], F32, tag="act", bufs=2)
@@ -177,85 +173,92 @@ def tile_routed_moe_kernel(tc, xT, w1, w3, w2, gate, offs, out):
         def project(e, nb0, nb1):
             c2, s2 = down_codes[e]
             hc, hs = h_codes[e]
-            y = psum.tile([P, NB, C], F32, tag="y", bufs=2)
+            y = psum.tile([P, NB, C], F32, tag="y", bufs=Y_BUFS)
             for nb in range(nb0, nb1):
                 for u in range(U):
                     cols = slice(u * N + nb * P, u * N + (nb + 1) * P)
                     h = slice(u * C, (u + 1) * C)
                     multiply(y[:, nb, :], c2[:, cols], s2[:, cols], hc[:, h], hs[:, h], u == 0, u == U - 1)
-            y_of[e] = y
+            for nb in range(nb0, nb1):
+                y_of[e, nb] = y
 
         def copy_out(e, nb0, nb1):
             slots = slice(e * C, (e + 1) * C)
-            ys = work.tile([P, NB, C], F32, tag="ys", bufs=2)
-            nc.vector.tensor_tensor(ys[:, nb0:nb1, :], y_of[e][:, nb0:nb1, :], gates[:, nb0:nb1, slots], MULT)
-            ys_of[e] = ys
+            ys = work.tile([P, NB, C], F32, tag="ys", bufs=3)
+            nc.scalar.copy(out=ys[:, nb0:nb1, :], in_=y_of[e, nb0][:, nb0:nb1, :])
+            for nb in range(nb0, nb1):
+                ys_of[e, nb] = ys
 
         def scatter(e, nb0, nb1):
             slots = slice(e * C, (e + 1) * C)
             for nb in range(nb0, nb1):
                 window = windows[nb][:].indirect(offsets[:, e * C // 16:(e + 1) * C // 16])
-                nc.vector.tensor_copy(window, ys_of[e][:, nb, :])
+                nc.vector.tensor_tensor(window, ys_of[e, nb][:, nb, :], gates[:, nb, slots], MULT)
                 if e == E - 1:
                     nc.sync.dma_start(out=out[nb * P:(nb + 1) * P, :], in_=windows[nb][:])
 
-        BOTH = (0, 1)
-        for e in range(E - 1):
-            cast_up(e, 0, BOTH, "S", 64, 256)
-            cast_up(e, 0, BOTH, "V", 0, 64)
-            if e > 0:
+        def cast_down_shared(e, u, n0, n1, share):
+            if n0 + share < n1:
+                cast_down(e, "S", u, n0 + share, n1)
+            if share:
+                cast_down(e, "V", u, n0, n0 + share)
+
+        for e in range(E):
+            last = e == E - 1
+            if e == 0:
+                cast_x(0)
+                quantize_x(0)
+                cast_up(0, 0, 0)
+                quantize_up(0, 0, 0)
+                cast_x(1)
+                quantize_x(1)
+                cast_up(0, 1, 0)
+                nc.vector.tensor_copy(g_codes[:], x_codes[:].indirect(offsets[:]))
+                nc.vector.tensor_copy(g_scales[:], x_scales[:].indirect(offsets[:]))
+                multiply_up(0, 0, 0)
+                activate(0, 0)
+                cast_up(0, 0, 1)
+                quantize_up(0, 1, 0)
+                multiply_up(0, 1, 0)
+            else:
+                cast_up(e, 0, 0)
                 copy_out(e - 1, 0, NB)
-            cast_up(e, 1, BOTH, "S", 64, 256)
-            quantize_up(e, 0, BOTH)
-            if e > 0:
-                scatter(e - 1, 0, NB)
-            cast_up(e, 1, BOTH, "V", 0, 64)
-            quantize_up(e, 1, BOTH)
-            multiply_up(e, 0)
-            multiply_up(e, 1)
-            cast_down(e, "S", 0, 0, N)
-            cast_down(e, "V", 1, 0, 128)
-            cast_down(e, "S", 1, 128, N)
-            activate(e, 0)
-            activate(e, 1)
-            quantize_down(e, 0, 512)
-            quantize_down(e, 512, 768)
+                quantize_up(e, 0, 0)
+                multiply_up(e, 0, 0)
+                cast_up(e, 1, 0)
+                scatter(e - 1, 0, 2)
+                activate(e, 0)
+                quantize_up(e, 1, 0)
+                multiply_up(e, 1, 0)
+                cast_up(e, 0, 1)
+                scatter(e - 1, 2, NB)
+            quantize_up(e, 0, 1)
+            multiply_up(e, 0, 1)
+            cast_up(e, 1, 1)
             gate_hidden(e, 0)
-            gate_hidden(e, 1)
-            quantize_hidden(e, 0, 2)
-            project(e, 0, NB)
-
-        e = E - 1
-
-        def cast_half(m, u):
-            cast_up(e, m, (u,), "S", 48, P)
-            cast_up(e, m, (u,), "V", 0, 48)
-
-        cast_half(0, 0)
-        copy_out(e - 1, 0, NB)
-        quantize_up(e, 0, (0,))
-        cast_half(1, 0)
-        scatter(e - 1, 0, NB)
-        quantize_up(e, 1, (0,))
-        multiply_up(e, 0)
-        cast_half(0, 1)
-        activate(e, 0)
-        quantize_up(e, 0, (1,))
-        gate_hidden(e, 0)
-        quantize_hidden(e, 0, 1)
-        cast_half(1, 1)
-        quantize_up(e, 1, (1,))
-        multiply_up(e, 1)
-        cast_down(e, "S", 0, 0, N)
-        activate(e, 1)
-        quantize_down(e, 0, 256)
-        quantize_down(e, 256, 384)
-        gate_hidden(e, 1)
-        quantize_hidden(e, 1, 2)
-        cast_down(e, "S", 1, 0, 192)
-        cast_down(e, "V", 1, 192, N)
-        quantize_down(e, 384, 640)
-        quantize_down(e, 640, 768)
-        project(e, 0, NB)
-        copy_out(e, 0, NB)
-        scatter(e, 0, NB)
+            cast_down_shared(e, 0, 0, N, LAST_SHARE[0] if last else DOWN_SHARE[0])
+            activate(e, 1)
+            quantize_up(e, 1, 1)
+            multiply_up(e, 1, 1)
+            quantize_hidden(e, 0, 1)
+            if not last:
+                cast_down_shared(e, 1, 0, N, DOWN_SHARE[1])
+                gate_hidden(e, 1)
+                quantize_down(e, 0, 512)
+                quantize_hidden(e, 1, 2)
+                quantize_down(e, 512, 768)
+                project(e, 0, NB)
+            else:
+                cast_down_shared(e, 1, 0, 256, LAST_SHARE[1])
+                quantize_down(e, 0, 256)
+                quantize_down(e, 256, 384)
+                gate_hidden(e, 1)
+                quantize_down(e, 384, 640)
+                quantize_hidden(e, 1, 2)
+                cast_down_shared(e, 1, 256, N, LAST_SHARE[2])
+                quantize_down(e, 640, 768)
+                for nb in range(NB):
+                    project(e, nb, nb + 1)
+                    copy_out(e, nb, nb + 1)
+                for nb in range(NB):
+                    scatter(e, nb, nb + 1)

@@ -19,9 +19,9 @@ U16 = mybir.dt.uint16
 U8 = mybir.dt.uint8
 X4 = mybir.dt.float8_e4m3fn_x4
 MULT = mybir.AluOpType.mult
-V_SHARE = [40,40,40,40]
 DOWN_SHARE = [0,384]
-LAST_SHARE = [0,128,64]
+LAST_SHARE = [0,128,128]
+DOWN_BUFS = {(0, 0): 2, (1, 0): 2, (1, 256): 1}
 Y_BUFS = 4
 SILU = mybir.ActivationFunctionType.Silu
 
@@ -72,9 +72,9 @@ def tile_routed_moe_kernel(tc, xT, w1, w3, w2, gate, offs, out):
             up_raw[e, m, u] = t
 
         def load_down(e, u, n0, n1):
-            if e not in down_raw:
-                down_raw[e] = raw.tile([P, U, PACK, N], F32, tag="down", bufs=2, name="down_r")
-            nc.sync.dma_start(out=down_raw[e][:, u, :, n0:n1], in_=w2[e].rearrange("(u p j) n -> p u j n", u=U, j=PACK)[:, u, :, n0:n1])
+            t = raw.tile([P, PACK, n1 - n0], F32, tag=f"down{u}{n0}", bufs=DOWN_BUFS[u, n0])
+            nc.sync.dma_start(out=t[:], in_=w2[e].rearrange("(u p j) n -> p u j n", u=U, j=PACK)[:, u, :, n0:n1])
+            down_raw[e, u, n0] = t
 
         load_x(0, 256)
         nc.sync.dma_start(offsets[:], offs)
@@ -117,10 +117,8 @@ def tile_routed_moe_kernel(tc, xT, w1, w3, w2, gate, offs, out):
         def cast_up(e, m, u):
             b = work.tile([P, PACK, P, PACK], BF16, tag="up_b", bufs=6, align_bytes=64)
             t = up_raw[e, m, u]
-            share = V_SHARE[e]
-            for eng, m0, m1 in (("S", share, P), ("V", 0, share)):
-                cast(eng, b[:, :, m0:m1, :].rearrange("p t m j -> p m j t"),
-                     t[:, :, 4 * m0:4 * m1].rearrange("p j (m t) -> p m j t", t=4))
+            eng = "V" if (m, u) == (0, 1) else "S"
+            cast(eng, b[:].rearrange("p t m j -> p m j t"), t[:].rearrange("p j (m t) -> p m j t", t=4))
             up_b[e, m, u] = b
 
         def quantize_up(e, m, u):
@@ -158,9 +156,11 @@ def tile_routed_moe_kernel(tc, xT, w1, w3, w2, gate, offs, out):
         def cast_down(e, eng, u, n0, n1):
             if e not in down_b:
                 down_b[e] = work.tile([P, U * N, PACK], BF16, tag="down_b", bufs=2, align_bytes=64, name="down_bt")
+            base = 256 if (e, u) == (E - 1, 1) and n0 >= 256 else 0
+            raw_t = down_raw[e, u, base]
             if n1 > n0:
                 cast(eng, down_b[e][:, u * N + n0:u * N + n1, :].rearrange("p (c i) j -> p c j i", i=4),
-                     down_raw[e][:, u, :, n0:n1].rearrange("p j (c i) -> p c j i", i=4))
+                     raw_t[:, :, n0 - base:n1 - base].rearrange("p j (c i) -> p c j i", i=4))
 
         def quantize_down(e, a0, a1):
             if e not in down_codes:

@@ -19,79 +19,85 @@ U16 = mybir.dt.uint16
 U8 = mybir.dt.uint8
 X4 = mybir.dt.float8_e4m3fn_x4
 MULT = mybir.AluOpType.mult
-DOWN_SHARE = [0,384]
-LAST_SHARE = [0,128,128]
-DOWN_BUFS = {(0, 0): 2, (1, 0): 2, (1, 256): 1}
-Y_BUFS = 4
 SILU = mybir.ActivationFunctionType.Silu
+VECTOR_TILES = {(0, 0): 4, (1, 0): 2}
+LAST_VECTOR_TILES = {(0, 0): 4, (1, 1): 2}
+
 
 def tile_routed_moe_kernel(tc, xT, w1, w3, w2, gate, offs, out):
     nc = tc.nc
+    last = E - 1
     with ExitStack() as ctx:
         held = ctx.enter_context(tc.tile_pool(name="held", bufs=1))
-        raw = ctx.enter_context(tc.tile_pool(name="raw", bufs=1))
-        work = ctx.enter_context(tc.tile_pool(name="work", bufs=1))
-        psum = ctx.enter_context(tc.psum_pool(name="psum", bufs=1))
+        raw = ctx.enter_context(tc.tile_pool(name="raw", bufs=2))
+        work = ctx.enter_context(tc.tile_pool(name="work", bufs=2))
+        psum = ctx.enter_context(tc.psum_pool(name="psum", bufs=2))
 
         offsets = held.tile([P, S // 16], U16, name="offsets")
         x_codes = held.tile([P, T], U32, name="x_codes", align_bytes=64)
         x_scales = held.tile([P, T], U8, name="x_scales", align_bytes=64)
         g_codes = held.tile([P, S], U32, name="g_codes", align_bytes=64)
         g_scales = held.tile([P, S], U8, name="g_scales", align_bytes=64)
-        gates = held.tile([P, NB, S], F32, name="gates")
         warm = held.tile([P, 1], F32, name="warm")
         windows = [held.tile([P, T], F32, name=f"window{b}") for b in range(NB)]
 
-        def cast(engine, dst, src):
+        def cast(engine, out, in_):
             if engine == "V":
-                nc.vector.tensor_copy(out=dst, in_=src)
+                nc.vector.tensor_copy(out=out, in_=in_)
             else:
-                nc.scalar.copy(out=dst, in_=src)
+                nc.scalar.copy(out=out, in_=in_)
 
         def quantize(codes, scales, grouped):
             nc.vector.quantize_mx(out=codes.bitcast(X4), scales=scales, in_=grouped)
 
-        def multiply(dst, l_codes, l_scales, r_codes, r_scales, start, stop):
-            nc.tensor.matmul_mx(out=dst, lhsT=l_codes.bitcast(X4), lhsT_scale=l_scales,
-                                rhs=r_codes.bitcast(X4), rhs_scale=r_scales, start=start, stop=stop)
+        def multiply(dst, left, right, start=True, stop=True):
+            nc.tensor.matmul_mx(out=dst, lhsT=left[0].bitcast(X4), lhsT_scale=left[1],
+                                rhs=right[0].bitcast(X4), rhs_scale=right[1], start=start, stop=stop)
 
-        x_view = xT.rearrange("(p j) n -> p j n", j=PACK)
-        x_parts = [(0, 256, [("V", 0, 256)]), (256, 512, [("S", 256, 512), ("V", 0, 256)])]
-        x_raw = []
+        up_raw, down_raw, gates = {}, {}, {}
 
-        def load_x(n0, width):
-            t = raw.tile([P, PACK, width], F32, name=f"x_raw{n0}")
-            nc.sync.dma_start(out=t[:], in_=x_view[:, :, n0:n0 + width])
-            x_raw.append(t)
+        def up_view(e, m):
+            return (w1, w3)[m][e].rearrange("(p j) c -> p j c", j=PACK)
 
-        up_raw, down_raw = {}, {}
+        def load_up(e, m):
+            t = raw.tile([P, PACK, H], F32, tag="up", bufs=5)
+            nc.sync.dma_start(out=t[:], in_=up_view(e, m))
+            for u in range(U):
+                up_raw[e, m, u] = t[:, :, u * HB:(u + 1) * HB]
 
-        def load_up(e, m, u):
-            t = raw.tile([P, PACK, HB], F32, tag="up", bufs=10)
-            nc.sync.dma_start(out=t[:], in_=(w1, w3)[m][e].rearrange("(p j) c -> p j c", j=PACK)[:, :, u * HB:(u + 1) * HB])
-            up_raw[e, m, u] = t
+        def load_up_half(e, m, u):
+            t = raw.tile([P, PACK, HB], F32, tag="up_half")
+            nc.sync.dma_start(out=t[:], in_=up_view(e, m)[:, :, u * HB:(u + 1) * HB])
+            up_raw[e, m, u] = t[:]
 
         def load_down(e, u, n0, n1):
-            t = raw.tile([P, PACK, n1 - n0], F32, tag=f"down{u}{n0}", bufs=DOWN_BUFS[u, n0])
+            t = raw.tile([P, PACK, n1 - n0], F32, tag=f"down{u}{n0}", bufs=1 if n0 else 2)
             nc.sync.dma_start(out=t[:], in_=w2[e].rearrange("(u p j) n -> p u j n", u=U, j=PACK)[:, u, :, n0:n1])
             down_raw[e, u, n0] = t
 
-        load_x(0, 256)
+        def load_gate(e0, e1):
+            t = held.tile([P, NB, (e1 - e0) * C], F32, name=f"gate{e0}")
+            nc.sync.dma_start(out=t[:], in_=gate.rearrange("(b p) s -> p b s", p=P)[:, :, e0 * C:e1 * C])
+            for e in range(e0, e1):
+                gates[e] = t[:, :, (e - e0) * C:(e - e0 + 1) * C]
+
+        x_raw = raw.tile([P, PACK, T], F32, tag="up", bufs=5)
+        nc.sync.dma_start(out=x_raw[:], in_=xT.rearrange("(p j) n -> p j n", j=PACK))
         nc.sync.dma_start(offsets[:], offs)
-        for e in range(E):
-            for u in range(U):
-                for m in range(2):
-                    load_up(e, m, u)
-                    if (e, m, u) == (0, 0, 0):
-                        load_x(256, 512)
-            if e == 0:
-                nc.sync.dma_start(out=gates[:], in_=gate.rearrange("(b p) s -> p b s", p=P))
+        for e in range(last):
+            load_up(e, 0)
+            load_up(e, 1)
+            if e > 0:
+                load_gate(e - 1, e)
             load_down(e, 0, 0, N)
-            if e < E - 1:
-                load_down(e, 1, 0, N)
-            else:
-                load_down(e, 1, 0, 256)
-                load_down(e, 1, 256, N)
+            load_down(e, 1, 0, N)
+        load_up(last, 0)
+        load_up_half(last, 1, 0)
+        load_gate(last - 1, E)
+        load_up_half(last, 1, 1)
+        load_down(last, 0, 0, N)
+        load_down(last, 1, 0, 256)
+        load_down(last, 1, 256, N)
 
         nc.vector.memset(warm[:], 0.0)
         nc.scalar.activation(out=warm[:], in_=warm[:], func=SILU)
@@ -99,166 +105,137 @@ def tile_routed_moe_kernel(tc, xT, w1, w3, w2, gate, offs, out):
         for window in windows:
             nc.vector.memset(window[:], 0.0)
 
-        x_b = []
+        for n0, n1, shares in ((0, 256, (("V", 0, 256),)), (256, 768, (("V", 256, 512), ("S", 512, 768)))):
+            xb = work.tile([P, n1 - n0, PACK], BF16, name=f"x_b{n0}", bufs=1, align_bytes=64)
+            for engine, a, b in shares:
+                cast(engine, xb[:, a - n0:b - n0, :].rearrange("p (c i) j -> p c j i", i=4), x_raw[:, :, a:b].rearrange("p j (c i) -> p c j i", i=4))
+            quantize(x_codes[:, n0:n1], x_scales[:, n0:n1], xb[:].rearrange("p n j -> p (n j)"))
+        nc.vector.tensor_copy(g_codes[:], x_codes[:].indirect(offsets[:]))
+        nc.vector.tensor_copy(g_scales[:], x_scales[:].indirect(offsets[:]))
 
-        def cast_x(i):
-            n0, width, shares = x_parts[i]
-            xb = work.tile([P, width, PACK], BF16, name=f"x_b{n0}", align_bytes=64)
-            for which, a, b in shares:
-                cast(which, xb[:, a:b, :].rearrange("p (c i) j -> p c j i", i=4), x_raw[i][:, :, a:b].rearrange("p j (c i) -> p c j i", i=4))
-            x_b.append(xb)
+        up_b, up_codes, banks, acts, h_b, h_codes, down_b, down_codes, y_of, ys_of = {}, {}, {}, {}, {}, {}, {}, {}, {}, {}
 
-        def quantize_x(i):
-            n0, width, shares = x_parts[i]
-            quantize(x_codes[:, n0:n0 + width], x_scales[:, n0:n0 + width], x_b[i][:].rearrange("p n j -> p (n j)"))
-
-        up_codes, banks, acts, h_groups, h_codes, down_codes, down_b, up_b, ys_of, y_of = {}, {}, {}, {}, {}, {}, {}, {}, {}, {}
+        def vector_tiles(e, m, u):
+            return (VECTOR_TILES if e < last else LAST_VECTOR_TILES).get((m, u), 0)
 
         def cast_up(e, m, u):
             b = work.tile([P, PACK, P, PACK], BF16, tag="up_b", bufs=6, align_bytes=64)
-            t = up_raw[e, m, u]
-            eng = "V" if (m, u) == (0, 1) else "S"
-            cast(eng, b[:].rearrange("p t m j -> p m j t"), t[:].rearrange("p j (m t) -> p m j t", t=4))
+            cut = PACK - vector_tiles(e, m, u)
+            for engine, t0, t1 in (("S", 0, cut), ("V", cut, PACK)):
+                if t0 < t1:
+                    cast(engine, b[:, t0:t1].rearrange("p t m j -> p m j t"),
+                         up_raw[e, m, u].rearrange("p j (m t) -> p m j t", t=PACK)[:, :, :, t0:t1])
             up_b[e, m, u] = b
 
         def quantize_up(e, m, u):
-            codes = work.tile([P, HB], U32, tag=f"c{m}{u}", bufs=2, align_bytes=64)
-            scales = work.tile([P, HB], U8, tag=f"s{m}{u}", bufs=2, align_bytes=64)
+            codes = work.tile([P, HB], U32, tag=f"codes{m}{u}", align_bytes=64)
+            scales = work.tile([P, HB], U8, tag=f"scales{m}{u}", align_bytes=64)
             quantize(codes[:], scales[:], up_b[e, m, u][:].rearrange("p t m j -> p (t m j)"))
             up_codes[e, m, u] = codes, scales
 
         def multiply_up(e, m, u):
             slots = slice(e * C, (e + 1) * C)
-            bank = psum.tile([P, PACK, C], F32, tag=f"bank{m}", bufs=2)
+            bank = psum.tile([P, PACK, C], F32, tag=f"bank{m}")
             codes, scales = up_codes[e, m, u]
             for t in range(PACK):
                 cols = slice(t * P, (t + 1) * P)
-                multiply(bank[:, t, :], codes[:, cols], scales[:, cols], g_codes[:, slots], g_scales[:, slots], True, True)
+                multiply(bank[:, t, :], (codes[:, cols], scales[:, cols]), (g_codes[:, slots], g_scales[:, slots]))
             banks[e, m, u] = bank
 
         def activate(e, u):
-            act = work.tile([P, C, PACK], F32, tag="act", bufs=2)
+            act = work.tile([P, C, PACK], F32, tag="act")
             nc.scalar.activation(out=act[:], in_=banks[e, 0, u][:].rearrange("p t n -> p n t"), func=SILU)
             acts[e, u] = act
 
-        def gate_hidden(e, u):
-            if e not in h_groups:
-                h_groups[e] = work.tile([P, U, C, PACK], BF16, tag="hb", bufs=2, align_bytes=64, name="hb")
-                codes = work.tile([P, U * C], U32, tag="hc", bufs=2, align_bytes=64)
-                scales = work.tile([P, U * C], U8, tag="hs", bufs=2, align_bytes=64)
-                h_codes[e] = codes, scales
-            nc.vector.tensor_tensor(h_groups[e][:, u], banks[e, 1, u][:].rearrange("p t n -> p n t"), acts[e, u][:], MULT)
+        def hidden(e, u):
+            b = work.tile([P, C, PACK], BF16, tag="h_b", align_bytes=64)
+            nc.vector.tensor_tensor(b[:], banks[e, 1, u][:].rearrange("p t n -> p n t"), acts[e, u][:], MULT)
+            h_b[e, u] = b
 
-        def quantize_hidden(e, u0, u1):
-            codes, scales = h_codes[e]
-            quantize(codes[:, u0 * C:u1 * C], scales[:, u0 * C:u1 * C], h_groups[e][:, u0:u1].rearrange("p u n t -> p (u n t)"))
+        def quantize_hidden(e, u):
+            codes = work.tile([P, C], U32, tag=f"h_codes{u}", align_bytes=64)
+            scales = work.tile([P, C], U8, tag=f"h_scales{u}", align_bytes=64)
+            quantize(codes[:], scales[:], h_b[e, u][:].rearrange("p n t -> p (n t)"))
+            h_codes[e, u] = codes[:], scales[:]
 
-        def cast_down(e, eng, u, n0, n1):
+        def cast_down(e, engine, u, n0, n1, base=0):
             if e not in down_b:
-                down_b[e] = work.tile([P, U * N, PACK], BF16, tag="down_b", bufs=2, align_bytes=64, name="down_bt")
-            base = 256 if (e, u) == (E - 1, 1) and n0 >= 256 else 0
-            raw_t = down_raw[e, u, base]
-            if n1 > n0:
-                cast(eng, down_b[e][:, u * N + n0:u * N + n1, :].rearrange("p (c i) j -> p c j i", i=4),
-                     raw_t[:, :, n0 - base:n1 - base].rearrange("p j (c i) -> p c j i", i=4))
+                down_b[e] = work.tile([P, U * N, PACK], BF16, tag="down_b", name="down_t", align_bytes=64)
+            cast(engine, down_b[e][:, u * N + n0:u * N + n1, :].rearrange("p (c i) j -> p c j i", i=4),
+                 down_raw[e, u, base][:, :, n0 - base:n1 - base].rearrange("p j (c i) -> p c j i", i=4))
 
-        def quantize_down(e, a0, a1):
+        def quantize_down(e, a, b):
             if e not in down_codes:
-                c2 = work.tile([P, U * N], U32, tag="c2", bufs=2, align_bytes=64)
-                s2 = work.tile([P, U * N], U8, tag="s2", bufs=2, align_bytes=64)
-                down_codes[e] = c2, s2
-            c2, s2 = down_codes[e]
-            quantize(c2[:, a0:a1], s2[:, a0:a1], down_b[e][:, a0:a1, :].rearrange("p n j -> p (n j)"))
+                codes = work.tile([P, U * N], U32, tag="down_codes", align_bytes=64)
+                scales = work.tile([P, U * N], U8, tag="down_scales", align_bytes=64)
+                down_codes[e] = codes, scales
+            codes, scales = down_codes[e]
+            quantize(codes[:, a:b], scales[:, a:b], down_b[e][:, a:b, :].rearrange("p n j -> p (n j)"))
 
-        def project(e, nb0, nb1):
-            c2, s2 = down_codes[e]
-            hc, hs = h_codes[e]
-            y = psum.tile([P, NB, C], F32, tag="y", bufs=Y_BUFS)
-            for nb in range(nb0, nb1):
+        def project(e, b0, b1):
+            codes, scales = down_codes[e]
+            y = psum.tile([P, NB, C], F32, tag="y", bufs=4)
+            for b in range(b0, b1):
                 for u in range(U):
-                    cols = slice(u * N + nb * P, u * N + (nb + 1) * P)
-                    h = slice(u * C, (u + 1) * C)
-                    multiply(y[:, nb, :], c2[:, cols], s2[:, cols], hc[:, h], hs[:, h], u == 0, u == U - 1)
-            for nb in range(nb0, nb1):
-                y_of[e, nb] = y
+                    cols = slice(u * N + b * P, u * N + (b + 1) * P)
+                    multiply(y[:, b, :], (codes[:, cols], scales[:, cols]), h_codes[e, u], u == 0, u == U - 1)
+            y_of[e, b0] = y
 
-        def copy_out(e, nb0, nb1):
-            slots = slice(e * C, (e + 1) * C)
+        def weigh(e, b0, b1):
             ys = work.tile([P, NB, C], F32, tag="ys", bufs=3)
-            nc.scalar.copy(out=ys[:, nb0:nb1, :], in_=y_of[e, nb0][:, nb0:nb1, :])
-            for nb in range(nb0, nb1):
-                ys_of[e, nb] = ys
+            nc.vector.tensor_tensor(ys[:, b0:b1, :], y_of[e, b0][:, b0:b1, :], gates[e][:, b0:b1, :], MULT)
+            for b in range(b0, b1):
+                ys_of[e, b] = ys
 
-        def scatter(e, nb0, nb1):
-            slots = slice(e * C, (e + 1) * C)
-            for nb in range(nb0, nb1):
-                window = windows[nb][:].indirect(offsets[:, e * C // 16:(e + 1) * C // 16])
-                nc.vector.tensor_tensor(window, ys_of[e, nb][:, nb, :], gates[:, nb, slots], MULT)
-                if e == E - 1:
-                    nc.sync.dma_start(out=out[nb * P:(nb + 1) * P, :], in_=windows[nb][:])
-
-        def cast_down_shared(e, u, n0, n1, share):
-            if n0 + share < n1:
-                cast_down(e, "S", u, n0 + share, n1)
-            if share:
-                cast_down(e, "V", u, n0, n0 + share)
+        def scatter(e, b0, b1):
+            for b in range(b0, b1):
+                nc.vector.tensor_copy(windows[b][:].indirect(offsets[:, e * C // 16:(e + 1) * C // 16]), ys_of[e, b][:, b, :])
+                if e == last:
+                    nc.sync.dma_start(out=out[b * P:(b + 1) * P, :], in_=windows[b][:])
 
         for e in range(E):
-            last = e == E - 1
-            if e == 0:
-                cast_x(0)
-                quantize_x(0)
-                cast_up(0, 0, 0)
-                quantize_up(0, 0, 0)
-                cast_x(1)
-                quantize_x(1)
-                cast_up(0, 1, 0)
-                nc.vector.tensor_copy(g_codes[:], x_codes[:].indirect(offsets[:]))
-                nc.vector.tensor_copy(g_scales[:], x_scales[:].indirect(offsets[:]))
-                multiply_up(0, 0, 0)
-                activate(0, 0)
-                cast_up(0, 0, 1)
-                quantize_up(0, 1, 0)
-                multiply_up(0, 1, 0)
-            else:
-                cast_up(e, 0, 0)
-                copy_out(e - 1, 0, NB)
-                quantize_up(e, 0, 0)
-                multiply_up(e, 0, 0)
-                cast_up(e, 1, 0)
+            cast_up(e, 0, 0)
+            if e > 0:
+                weigh(e - 1, 0, NB)
+            quantize_up(e, 0, 0)
+            multiply_up(e, 0, 0)
+            cast_up(e, 0, 1)
+            activate(e, 0)
+            if e > 0:
                 scatter(e - 1, 0, 2)
-                activate(e, 0)
-                quantize_up(e, 1, 0)
-                multiply_up(e, 1, 0)
-                cast_up(e, 0, 1)
-                scatter(e - 1, 2, NB)
             quantize_up(e, 0, 1)
             multiply_up(e, 0, 1)
-            cast_up(e, 1, 1)
-            gate_hidden(e, 0)
-            cast_down_shared(e, 0, 0, N, LAST_SHARE[0] if last else DOWN_SHARE[0])
             activate(e, 1)
+            if e > 0:
+                scatter(e - 1, 2, NB)
+            cast_up(e, 1, 0)
+            quantize_up(e, 1, 0)
+            multiply_up(e, 1, 0)
+            cast_up(e, 1, 1)
+            hidden(e, 0)
             quantize_up(e, 1, 1)
             multiply_up(e, 1, 1)
-            quantize_hidden(e, 0, 1)
-            if not last:
-                cast_down_shared(e, 1, 0, N, DOWN_SHARE[1])
-                gate_hidden(e, 1)
+            quantize_hidden(e, 0)
+            cast_down(e, "S", 0, 0, N)
+            if e < last:
+                cast_down(e, "V", 1, 0, 192)
+                cast_down(e, "S", 1, 192, N)
+                hidden(e, 1)
                 quantize_down(e, 0, 512)
-                quantize_hidden(e, 1, 2)
+                quantize_hidden(e, 1)
                 quantize_down(e, 512, 768)
                 project(e, 0, NB)
             else:
-                cast_down_shared(e, 1, 0, 256, LAST_SHARE[1])
+                cast_down(e, "S", 1, 0, 256)
                 quantize_down(e, 0, 256)
                 quantize_down(e, 256, 384)
-                gate_hidden(e, 1)
+                hidden(e, 1)
                 quantize_down(e, 384, 640)
-                quantize_hidden(e, 1, 2)
-                cast_down_shared(e, 1, 256, N, LAST_SHARE[2])
+                quantize_hidden(e, 1)
+                cast_down(e, "S", 1, 256, N, 256)
                 quantize_down(e, 640, 768)
-                for nb in range(NB):
-                    project(e, nb, nb + 1)
-                    copy_out(e, nb, nb + 1)
-                for nb in range(NB):
-                    scatter(e, nb, nb + 1)
+                for b in range(NB):
+                    project(e, b, b + 1)
+                    weigh(e, b, b + 1)
+                for b in range(NB):
+                    scatter(e, b, b + 1)

from contextlib import ExitStack

import concourse.mybir as mybir

K, T, E, C, H, N = 512, 768, 4, 128, 1024, 384
S = E * C
P = 128
PACK = 4
HB = 512
U = H // HB
NB = N // P

FLOPS = 2 * K * H * S * 2 + 2 * H * N * S

F32 = mybir.dt.float32
BF16 = mybir.dt.bfloat16
U32 = mybir.dt.uint32
U16 = mybir.dt.uint16
U8 = mybir.dt.uint8
X4 = mybir.dt.float8_e4m3fn_x4
MULT = mybir.AluOpType.mult
SILU = mybir.ActivationFunctionType.Silu
VECTOR_TILES = {(0, 0): 4, (1, 0): 2}
LAST_VECTOR_TILES = {(0, 0): 4, (1, 1): 2}


def tile_routed_moe_kernel(tc, xT, w1, w3, w2, gate, offs, out):
    nc = tc.nc
    last = E - 1
    with ExitStack() as ctx:
        held = ctx.enter_context(tc.tile_pool(name="held", bufs=1))
        raw = ctx.enter_context(tc.tile_pool(name="raw", bufs=2))
        work = ctx.enter_context(tc.tile_pool(name="work", bufs=2))
        psum = ctx.enter_context(tc.psum_pool(name="psum", bufs=2))

        offsets = held.tile([P, S // 16], U16, name="offsets")
        x_codes = held.tile([P, T], U32, name="x_codes", align_bytes=64)
        x_scales = held.tile([P, T], U8, name="x_scales", align_bytes=64)
        g_codes = held.tile([P, S], U32, name="g_codes", align_bytes=64)
        g_scales = held.tile([P, S], U8, name="g_scales", align_bytes=64)
        warm = held.tile([P, 1], F32, name="warm")
        windows = [held.tile([P, T], F32, name=f"window{b}") for b in range(NB)]

        def cast(engine, out, in_):
            if engine == "V":
                nc.vector.tensor_copy(out=out, in_=in_)
            else:
                nc.scalar.copy(out=out, in_=in_)

        def quantize(codes, scales, grouped):
            nc.vector.quantize_mx(out=codes.bitcast(X4), scales=scales, in_=grouped)

        def multiply(dst, left, right, start=True, stop=True):
            nc.tensor.matmul_mx(out=dst, lhsT=left[0].bitcast(X4), lhsT_scale=left[1],
                                rhs=right[0].bitcast(X4), rhs_scale=right[1], start=start, stop=stop)

        up_raw, down_raw, gates = {}, {}, {}

        def up_view(e, m):
            return (w1, w3)[m][e].rearrange("(p j) c -> p j c", j=PACK)

        def load_up(e, m):
            t = raw.tile([P, PACK, H], F32, tag="up", bufs=5)
            nc.sync.dma_start(out=t[:], in_=up_view(e, m))
            for u in range(U):
                up_raw[e, m, u] = t[:, :, u * HB:(u + 1) * HB]

        def load_up_half(e, m, u):
            t = raw.tile([P, PACK, HB], F32, tag="up_half")
            nc.sync.dma_start(out=t[:], in_=up_view(e, m)[:, :, u * HB:(u + 1) * HB])
            up_raw[e, m, u] = t[:]

        def load_down(e, u, n0, n1):
            t = raw.tile([P, PACK, n1 - n0], F32, tag=f"down{u}{n0}", bufs=1 if n0 else 2)
            nc.sync.dma_start(out=t[:], in_=w2[e].rearrange("(u p j) n -> p u j n", u=U, j=PACK)[:, u, :, n0:n1])
            down_raw[e, u, n0] = t

        def load_gate(e0, e1):
            t = held.tile([P, NB, (e1 - e0) * C], F32, name=f"gate{e0}")
            nc.sync.dma_start(out=t[:], in_=gate.rearrange("(b p) s -> p b s", p=P)[:, :, e0 * C:e1 * C])
            for e in range(e0, e1):
                gates[e] = t[:, :, (e - e0) * C:(e - e0 + 1) * C]

        x_raw = raw.tile([P, PACK, T], F32, tag="up", bufs=5)
        nc.sync.dma_start(out=x_raw[:], in_=xT.rearrange("(p j) n -> p j n", j=PACK))
        nc.sync.dma_start(offsets[:], offs)
        for e in range(last):
            load_up(e, 0)
            load_up(e, 1)
            if e > 0:
                load_gate(e - 1, e)
            load_down(e, 0, 0, N)
            load_down(e, 1, 0, N)
        load_up(last, 0)
        load_up_half(last, 1, 0)
        load_gate(last - 1, E)
        load_up_half(last, 1, 1)
        load_down(last, 0, 0, N)
        load_down(last, 1, 0, 256)
        load_down(last, 1, 256, N)

        nc.vector.memset(warm[:], 0.0)
        nc.scalar.activation(out=warm[:], in_=warm[:], func=SILU)
        nc.gpsimd.memset(x_scales[:], 0)
        for window in windows:
            nc.vector.memset(window[:], 0.0)

        for n0, n1, shares in ((0, 256, (("V", 0, 256),)), (256, 768, (("V", 256, 512), ("S", 512, 768)))):
            xb = work.tile([P, n1 - n0, PACK], BF16, name=f"x_b{n0}", bufs=1, align_bytes=64)
            for engine, a, b in shares:
                cast(engine, xb[:, a - n0:b - n0, :].rearrange("p (c i) j -> p c j i", i=4), x_raw[:, :, a:b].rearrange("p j (c i) -> p c j i", i=4))
            quantize(x_codes[:, n0:n1], x_scales[:, n0:n1], xb[:].rearrange("p n j -> p (n j)"))
        nc.vector.tensor_copy(g_codes[:], x_codes[:].indirect(offsets[:]))
        nc.vector.tensor_copy(g_scales[:], x_scales[:].indirect(offsets[:]))

        up_b, up_codes, banks, acts, h_b, h_codes, down_b, down_codes, y_of, ys_of = {}, {}, {}, {}, {}, {}, {}, {}, {}, {}

        def vector_tiles(e, m, u):
            return (VECTOR_TILES if e < last else LAST_VECTOR_TILES).get((m, u), 0)

        def cast_up(e, m, u):
            b = work.tile([P, PACK, P, PACK], BF16, tag="up_b", bufs=6, align_bytes=64)
            cut = PACK - vector_tiles(e, m, u)
            for engine, t0, t1 in (("S", 0, cut), ("V", cut, PACK)):
                if t0 < t1:
                    cast(engine, b[:, t0:t1].rearrange("p t m j -> p m j t"),
                         up_raw[e, m, u].rearrange("p j (m t) -> p m j t", t=PACK)[:, :, :, t0:t1])
            up_b[e, m, u] = b

        def quantize_up(e, m, u):
            codes = work.tile([P, HB], U32, tag=f"codes{m}{u}", align_bytes=64)
            scales = work.tile([P, HB], U8, tag=f"scales{m}{u}", align_bytes=64)
            quantize(codes[:], scales[:], up_b[e, m, u][:].rearrange("p t m j -> p (t m j)"))
            up_codes[e, m, u] = codes, scales

        def multiply_up(e, m, u):
            slots = slice(e * C, (e + 1) * C)
            bank = psum.tile([P, PACK, C], F32, tag=f"bank{m}")
            codes, scales = up_codes[e, m, u]
            for t in range(PACK):
                cols = slice(t * P, (t + 1) * P)
                multiply(bank[:, t, :], (codes[:, cols], scales[:, cols]), (g_codes[:, slots], g_scales[:, slots]))
            banks[e, m, u] = bank

        def activate(e, u):
            act = work.tile([P, C, PACK], F32, tag="act")
            nc.scalar.activation(out=act[:], in_=banks[e, 0, u][:].rearrange("p t n -> p n t"), func=SILU)
            acts[e, u] = act

        def hidden(e, u):
            b = work.tile([P, C, PACK], BF16, tag="h_b", align_bytes=64)
            nc.vector.tensor_tensor(b[:], banks[e, 1, u][:].rearrange("p t n -> p n t"), acts[e, u][:], MULT)
            h_b[e, u] = b

        def quantize_hidden(e, u):
            codes = work.tile([P, C], U32, tag=f"h_codes{u}", align_bytes=64)
            scales = work.tile([P, C], U8, tag=f"h_scales{u}", align_bytes=64)
            quantize(codes[:], scales[:], h_b[e, u][:].rearrange("p n t -> p (n t)"))
            h_codes[e, u] = codes[:], scales[:]

        def cast_down(e, engine, u, n0, n1, base=0):
            if e not in down_b:
                down_b[e] = work.tile([P, U * N, PACK], BF16, tag="down_b", name="down_t", align_bytes=64)
            cast(engine, down_b[e][:, u * N + n0:u * N + n1, :].rearrange("p (c i) j -> p c j i", i=4),
                 down_raw[e, u, base][:, :, n0 - base:n1 - base].rearrange("p j (c i) -> p c j i", i=4))

        def quantize_down(e, a, b):
            if e not in down_codes:
                codes = work.tile([P, U * N], U32, tag="down_codes", align_bytes=64)
                scales = work.tile([P, U * N], U8, tag="down_scales", align_bytes=64)
                down_codes[e] = codes, scales
            codes, scales = down_codes[e]
            quantize(codes[:, a:b], scales[:, a:b], down_b[e][:, a:b, :].rearrange("p n j -> p (n j)"))

        def project(e, b0, b1):
            codes, scales = down_codes[e]
            y = psum.tile([P, NB, C], F32, tag="y", bufs=4)
            for b in range(b0, b1):
                for u in range(U):
                    cols = slice(u * N + b * P, u * N + (b + 1) * P)
                    multiply(y[:, b, :], (codes[:, cols], scales[:, cols]), h_codes[e, u], u == 0, u == U - 1)
            y_of[e, b0] = y

        def weigh(e, b0, b1):
            ys = work.tile([P, NB, C], F32, tag="ys", bufs=3)
            nc.vector.tensor_tensor(ys[:, b0:b1, :], y_of[e, b0][:, b0:b1, :], gates[e][:, b0:b1, :], MULT)
            for b in range(b0, b1):
                ys_of[e, b] = ys

        def scatter(e, b0, b1):
            for b in range(b0, b1):
                nc.vector.tensor_copy(windows[b][:].indirect(offsets[:, e * C // 16:(e + 1) * C // 16]), ys_of[e, b][:, b, :])
                if e == last:
                    nc.sync.dma_start(out=out[b * P:(b + 1) * P, :], in_=windows[b][:])

        for e in range(E):
            cast_up(e, 0, 0)
            if e > 0:
                weigh(e - 1, 0, NB)
            quantize_up(e, 0, 0)
            multiply_up(e, 0, 0)
            cast_up(e, 0, 1)
            activate(e, 0)
            if e > 0:
                scatter(e - 1, 0, 2)
            quantize_up(e, 0, 1)
            multiply_up(e, 0, 1)
            activate(e, 1)
            if e > 0:
                scatter(e - 1, 2, NB)
            cast_up(e, 1, 0)
            quantize_up(e, 1, 0)
            multiply_up(e, 1, 0)
            cast_up(e, 1, 1)
            hidden(e, 0)
            quantize_up(e, 1, 1)
            multiply_up(e, 1, 1)
            quantize_hidden(e, 0)
            cast_down(e, "S", 0, 0, N)
            if e < last:
                cast_down(e, "V", 1, 0, 192)
                cast_down(e, "S", 1, 192, N)
                hidden(e, 1)
                quantize_down(e, 0, 512)
                quantize_hidden(e, 1)
                quantize_down(e, 512, 768)
                project(e, 0, NB)
            else:
                cast_down(e, "S", 1, 0, 256)
                quantize_down(e, 0, 256)
                quantize_down(e, 256, 384)
                hidden(e, 1)
                quantize_down(e, 384, 640)
                quantize_hidden(e, 1)
                cast_down(e, "S", 1, 256, N, 256)
                quantize_down(e, 640, 768)
                for b in range(NB):
                    project(e, b, b + 1)
                    weigh(e, b, b + 1)
                for b in range(NB):
                    scatter(e, b, b + 1)
